import numpy as np
import ml_dtypes


def mxq(x, axis, fmt="e4m3"):
    dtype, down = {"e4m3": (ml_dtypes.float8_e4m3fn, 7), "e5m2": (ml_dtypes.float8_e5m2, 14)}[fmt]
    v = np.moveaxis(np.asarray(x, np.float32).astype(ml_dtypes.bfloat16).astype(np.float64), axis, -1)
    blocks = v.reshape(v.shape[:-1] + (-1, 32))
    amax = np.abs(blocks).max(-1, keepdims=True)
    byte = np.maximum(np.where(amax > 0, np.frexp(amax)[1] - 1 + 127, 0) - down, 1)
    scale = np.exp2(byte - 127.0)
    codes = (blocks / scale).astype(np.float32).astype(dtype).astype(np.float64)
    return np.moveaxis((codes * scale).reshape(v.shape), -1, axis)


WIDE = False


def mx_kscale(k):
    if not WIDE:
        return np.ones(k)
    levels = np.array([30, -30])
    if k % 512:
        return np.exp2(np.random.permutation(np.resize(levels, k // 32))).repeat(32)
    a = np.empty((k // 512, 16))
    for p in range(k // 512):
        a[p, :8] = np.random.permutation(np.resize(levels, 8))
        for g in range(8):
            far = levels[np.abs(levels - a[p, g]) >= 10]
            a[p, g + 8] = far[np.random.randint(len(far))]
    return np.exp2(a.ravel()).repeat(32)


def f64(x):
    return np.asarray(x).astype(np.float64)


def striped(idx):
    return np.tile(np.asarray(idx).reshape(-1, 16).T, (8, 1)).astype(np.uint16)


def unstriped(offs):
    return offs[:16].T.reshape(-1).astype(np.int64)


E2M1 = np.array([0.0, 0.5, 1.0, 1.5, 2.0, 3.0, 4.0, 6.0, -0.0, -0.5, -1.0, -1.5, -2.0, -3.0, -4.0, -6.0])


def pack_weight(w, fmt):
    k, n = w.shape
    w = f64(np.asarray(w, np.float32).astype(ml_dtypes.bfloat16)).reshape(k // 32, 32, n)
    amax = np.abs(w).max(1)
    if fmt in ("e4m3", "e5m2"):
        byte = np.frexp(amax)[1] - 1 + 127 - (7 if fmt == "e4m3" else 14)
    else:
        mant, ex = np.frexp(amax / 6.0)
        byte = np.where(mant > 0.5, ex, ex - 1) + 127
    byte = np.clip(np.where(amax > 0, byte, 1), 1, 254)
    scaled = (w * np.exp2(127.0 - byte)[:, None, :]).reshape(k, n).astype(np.float32)
    by_word = np.ascontiguousarray(scaled.reshape(k // 512, 128, 4, n).transpose(0, 1, 3, 2))
    if fmt in ("e4m3", "e5m2"):
        words = by_word.astype(ml_dtypes.float8_e4m3fn if fmt == "e4m3" else ml_dtypes.float8_e5m2).view(np.uint8)
    else:
        c = by_word.astype(ml_dtypes.float4_e2m1fn).view(np.uint8) & 0xF
        words = (c[..., 0::2] | (c[..., 1::2] << 4)).reshape(k // 512, 128, 2 * n)
    return np.ascontiguousarray(words), np.ascontiguousarray(byte.astype(np.uint8).reshape(k // 512, 16, n))


def unpack_weight(words, scales, fmt):
    g, _, n = scales.shape
    words = np.ascontiguousarray(words).reshape(g, 128, n, -1)
    if fmt in ("e4m3", "e5m2"):
        vals = words.view(ml_dtypes.float8_e4m3fn if fmt == "e4m3" else ml_dtypes.float8_e5m2).astype(np.float64)
    else:
        nib = np.empty((g, 128, n, 4), np.uint8)
        nib[..., 0::2] = words & 0xF
        nib[..., 1::2] = words >> 4
        vals = E2M1[nib]
    vals = vals * np.repeat(np.exp2(scales.astype(np.float64) - 127.0), 8, axis=1)[..., None]
    return vals.transpose(0, 1, 3, 2).reshape(g * 512, n)


K, T, J, R, I, O, N, S, E = 512, 1024, 256, 512, 256, 128, 256, 1024, 1024


def setup_inputs():
    n = np.random.standard_normal
    idx = np.random.permutation(T)[:J]
    idx2 = np.random.permutation(J)[:I]
    idx3 = np.random.permutation(J)[:I]
    idx4 = np.random.permutation(I)[:O]
    idx5 = np.random.permutation(I)[:O]
    idx6 = np.random.permutation(S)[:N]
    idx7 = np.random.permutation(E)[:O]
    fk = mx_kscale(K)
    fr = mx_kscale(R)
    xtp = pack_weight(n((K, T)) / fk[:, None], "e2m1")
    wp = pack_weight(n((K, R)) * 1 / np.sqrt(K) * fk[:, None] * fr, "e4m3")
    w2p = pack_weight(n((K, R)) * 1 / np.sqrt(K) * fk[:, None], "e5m2")
    vsp = pack_weight(n((R, S)) * 1 / np.sqrt(R) / fr[:, None], "e2m1")
    return {
        "xt_words": xtp[0],
        "xt_scales": xtp[1],
        "w_words": wp[0],
        "w_scales": wp[1],
        "w2_words": w2p[0],
        "w2_scales": w2p[1],
        "vs_words": vsp[0],
        "vs_scales": vsp[1],
        "offs": striped(idx),
        "offs2": striped(idx2),
        "offs3": striped(idx3),
        "offs4": striped(idx4),
        "offs5": striped(idx5),
        "offs6": striped(idx6),
        "offs7": striped(idx7),
    }


def reference(xt_words, xt_scales, w_words, w_scales, w2_words, w2_scales, vs_words, vs_scales, offs, offs2, offs3, offs4, offs5, offs6, offs7):
    idx = unstriped(offs)
    idx2 = unstriped(offs2)
    idx3 = unstriped(offs3)
    idx4 = unstriped(offs4)
    idx5 = unstriped(offs5)
    idx6 = unstriped(offs6)
    idx7 = unstriped(offs7)
    xtu = unpack_weight(xt_words, xt_scales, "e2m1")
    wu = unpack_weight(w_words, w_scales, "e4m3")
    w2u = unpack_weight(w2_words, w2_scales, "e5m2")
    vsu = unpack_weight(vs_words, vs_scales, "e2m1")
    xtidxg = xtu[:, idx]
    a = wu.T @ xtidxg
    b = w2u.T @ xtidxg
    lb = b[:, 0:1]
    la = a[:, 0:1]
    h1 = np.maximum(a[:, idx2] * lb, b[:, idx3] * la)
    hid = np.abs(h1[:, idx4] - h1[:, idx5])
    vsidx6g = vsu[:, idx6]
    hidq = mxq(hid, 0, "e5m2")
    p = vsidx6g.T @ hidq
    y = np.zeros((N, E))
    y[:, idx7] = p
    return y

@@ -1,0 +1,173 @@
+from contextlib import ExitStack
+
+import concourse.mybir as mybir
+
+K, T, J, R, I, O, N, S, E = 512, 1024, 256, 512, 256, 128, 256, 1024, 1024
+FLOPS = 2 * (2 * K * R * J + R * N * O)
+
+F32 = mybir.dt.float32
+BF16 = mybir.dt.bfloat16
+I32 = mybir.dt.int32
+U32 = mybir.dt.uint32
+U16 = mybir.dt.uint16
+U8 = mybir.dt.uint8
+E4M3 = mybir.dt.float8_e4m3fn_x4
+E5M2 = mybir.dt.float8_e5m2_x4
+E2M1 = mybir.dt.float4_e2m1fn_x4
+ACT = mybir.ActivationFunctionType
+ALU = mybir.AluOpType
+
+P = 128
+PACK = 4
+QUADS = 4
+QUAD = 32
+ROWS = 4
+WIDE = 512
+
+
+def tile_list_leadmeetthenlook_twow_store_scattered_kernel(
+    tc, xt_words, xt_scales, w_words, w_scales, w2_words, w2_scales, vs_words, vs_scales,
+    offs, offs2, offs3, offs4, offs5, offs6, offs7, out,
+):
+    nc = tc.nc
+    with ExitStack() as ctx:
+        lists = ctx.enter_context(tc.tile_pool(name="lists", bufs=1))
+        keep = ctx.enter_context(tc.tile_pool(name="keep", bufs=1))
+        psum = ctx.enter_context(tc.psum_pool(name="psum", bufs=1))
+
+        def load_list(src, name):
+            tile = lists.tile(list(src.shape), U16, name=name)
+            nc.sync.dma_start(tile[:], src)
+            return tile
+
+        def by_quad(scales):
+            return scales[0].bitcast(I32).rearrange("(q r) c -> r q c", r=ROWS)
+
+        xs_plane = keep.tile([P, T], U8, name="xs_plane", align_bytes=64)
+        ws_plane = keep.tile([P, 2, R], U8, name="ws_plane", align_bytes=64)
+        vs_plane = keep.tile([P, S], U8, name="vs_plane", align_bytes=64)
+        nc.vector.memset(xs_plane[:].bitcast(I32), 0)
+        nc.vector.memset(ws_plane[:].rearrange("p a c -> p (a c)").bitcast(I32), 0)
+        nc.vector.memset(vs_plane[:].bitcast(I32), 0)
+        pages = [keep.tile([P, E], F32, name="page%d" % c) for c in range(2)]
+        nc.vector.memset(pages[0][:], 0.0)
+        nc.gpsimd.memset(pages[1][:], 0.0)
+
+        xs_stage = keep.tile([P, 2, T // 4], I32, name="xs_stage")
+        for h in range(2):
+            nc.sync.dma_start(xs_stage[64 * h : 64 * h + ROWS, :, :], by_quad(xt_scales)[:, 2 * h : 2 * h + 2, :])
+        l1 = load_list(offs, "l1")
+        xt_sb = keep.tile([P, T], U16, name="xt_sb", align_bytes=64)
+        nc.sync.dma_start(xt_sb[:].bitcast(I32), xt_words[0].bitcast(I32))
+        ws_stage = keep.tile([ROWS, QUADS, 2, R // 4], I32, name="ws_stage")
+        nc.sync.dma_start(ws_stage[:, :, 0, :], by_quad(w_scales))
+        nc.sync.dma_start(ws_stage[:, :, 1, :], by_quad(w2_scales))
+        w_sb = keep.tile([P, R], U32, name="w_sb")
+        w2_sb = keep.tile([P, R], U32, name="w2_sb")
+        nc.sync.dma_start(w_sb[:].bitcast(I32), w_words[0].rearrange("p n t -> p (n t)").bitcast(I32))
+        nc.sync.dma_start(w2_sb[:].bitcast(I32), w2_words[0].rearrange("p n t -> p (n t)").bitcast(I32))
+        l2 = load_list(offs2, "l2")
+        l3 = load_list(offs3, "l3")
+        l6 = load_list(offs6, "l6")
+        vs_sb = keep.tile([P, S], U16, name="vs_sb", align_bytes=64)
+        nc.sync.dma_start(vs_sb[:].bitcast(I32), vs_words[0].bitcast(I32))
+        l4 = load_list(offs4, "l4")
+        l5 = load_list(offs5, "l5")
+        for q in range(QUADS):
+            nc.sync.dma_start(
+                vs_plane[QUAD * q : QUAD * q + ROWS, :].bitcast(I32),
+                vs_scales[0, ROWS * q : ROWS * q + ROWS, :].bitcast(I32),
+            )
+        l7 = load_list(offs7, "l7")
+
+        for q in range(QUADS):
+            src = 64 * (q // 2)
+            nc.vector.tensor_copy(
+                xs_plane[QUAD * q : QUAD * q + ROWS, :].bitcast(I32), xs_stage[src : src + ROWS, q % 2, :]
+            )
+        xg_scales = keep.tile([P, J], U8, name="xg_scales", align_bytes=64)
+        xg_words = keep.tile([P, J], U16, name="xg_words", align_bytes=64)
+        nc.vector.tensor_copy(xg_scales[:], xs_plane[:].indirect(l1[:]))
+        for q in range(QUADS):
+            nc.vector.tensor_copy(
+                ws_plane[QUAD * q : QUAD * q + ROWS, :, :].rearrange("p a c -> p (a c)").bitcast(I32),
+                ws_stage[:, q, :, :].rearrange("p a c -> p (a c)"),
+            )
+        nc.vector.tensor_copy(xg_words[:], xt_sb[:].indirect(l1[:]))
+
+        w_dealt = keep.tile([P, PACK, P], U32, name="w_dealt", align_bytes=64)
+        w2_dealt = keep.tile([P, PACK, P], U32, name="w2_dealt", align_bytes=64)
+        ws_dealt = keep.tile([P, PACK, 2, P], U8, name="ws_dealt", align_bytes=64)
+        nc.scalar.copy(w_dealt[:], w_sb[:].rearrange("p (m t) -> p t m", t=PACK))
+        w2_view = w2_sb[:].rearrange("p (m t) -> p t m", t=PACK)
+        nc.scalar.copy(w2_dealt[:, 0, :], w2_view[:, 0, :])
+        nc.scalar.copy(w2_dealt[:, 1:, :], w2_view[:, 1:, :])
+        ws_view = ws_plane[:].rearrange("p a (m t) -> p t a m", t=PACK)
+        nc.vector.tensor_copy(ws_dealt[:, 0, :, :], ws_view[:, 0, :, :])
+        nc.vector.tensor_copy(ws_dealt[:, 1:, :, :], ws_view[:, 1:, :, :])
+
+        a_sb, b_sb = [], []
+        for t in range(PACK):
+            a_ps = psum.tile([P, J], F32, name="a_ps%d" % t, tag="bank_a%d" % t)
+            b_ps = psum.tile([P, J], F32, name="b_ps%d" % t, tag="bank_b%d" % t)
+            nc.tensor.matmul_mx(
+                out=a_ps[:], lhsT=w_dealt[:, t, :].bitcast(E4M3), lhsT_scale=ws_dealt[:, t, 0, :],
+                rhs=xg_words[:].bitcast(E2M1), rhs_scale=xg_scales[:], start=True, stop=True,
+            )
+            nc.tensor.matmul_mx(
+                out=b_ps[:], lhsT=w2_dealt[:, t, :].bitcast(E5M2), lhsT_scale=ws_dealt[:, t, 1, :],
+                rhs=xg_words[:].bitcast(E2M1), rhs_scale=xg_scales[:], start=True, stop=True,
+            )
+            a_t = keep.tile([P, WIDE], F32, name="a_sb%d" % t)
+            b_t = keep.tile([P, WIDE], F32, name="b_sb%d" % t)
+            if t == 0:
+                nc.scalar.copy(a_t[:, :J], a_ps[:])
+            else:
+                nc.vector.tensor_copy(a_t[:, :J], a_ps[:])
+            nc.vector.tensor_copy(b_t[:, :J], b_ps[:])
+            a_sb.append(a_t)
+            b_sb.append(b_t)
+
+        vg_scales = keep.tile([P, N], U8, name="vg_scales", align_bytes=64)
+        vg_words = keep.tile([P, N], U16, name="vg_words", align_bytes=64)
+        nc.vector.tensor_copy(vg_words[:], vs_sb[:].indirect(l6[:]))
+
+        diff = keep.tile([P, PACK, O], F32, name="diff")
+        for t in range(PACK):
+            ga = keep.tile([P, I], F32, name="ga%d" % t)
+            gb = keep.tile([P, I], F32, name="gb%d" % t)
+            nc.scalar.activation(ga[:], a_sb[t][:].indirect(l2[:]), ACT.Copy, scale=b_sb[t][:, 0:1])
+            nc.scalar.activation(gb[:], b_sb[t][:].indirect(l3[:]), ACT.Copy, scale=a_sb[t][:, 0:1])
+            h1 = keep.tile([P, I], F32, name="h1_%d" % t)
+            nc.vector.tensor_tensor(h1[:], ga[:], gb[:], ALU.max)
+            first = keep.tile([P, O], F32, name="first%d" % t)
+            nc.vector.tensor_copy(first[:], h1[:].indirect(l4[:]))
+            nc.vector.tensor_tensor(diff[:, t, :], h1[:].indirect(l5[:]), first[:], ALU.subtract)
+
+        nc.vector.tensor_copy(vg_scales[:], vs_plane[:].indirect(l6[:]))
+
+        hid = keep.tile([P, O, PACK], BF16, name="hid", align_bytes=64)
+        nc.scalar.activation(
+            hid[:].rearrange("p (c i) t -> p c t i", i=4), diff[:].rearrange("p t (c i) -> p c t i", i=4), ACT.Abs
+        )
+        hid_words = keep.tile([P, O], U32, name="hid_words", align_bytes=64)
+        hid_scales = keep.tile([P, O], U8, name="hid_scales", align_bytes=64)
+        nc.vector.quantize_mx(
+            out=hid_words[:].bitcast(E5M2), scales=hid_scales[:], in_=hid[:].rearrange("p o t -> p (o t)")
+        )
+
+        for c in range(2):
+            cols = slice(c * P, (c + 1) * P)
+            p_ps = psum.tile([P, O], F32, name="p_ps%d" % c, tag="bank_a%d" % c)
+            nc.tensor.matmul_mx(
+                out=p_ps[:], lhsT=vg_words[:, cols].bitcast(E2M1), lhsT_scale=vg_scales[:, cols],
+                rhs=hid_words[:].bitcast(E5M2), rhs_scale=hid_scales[:], start=True, stop=True,
+            )
+            p_sb = keep.tile([P, O], F32, name="p_sb%d" % c)
+            if c == 0:
+                nc.vector.tensor_copy(p_sb[:], p_ps[:])
+                nc.vector.tensor_copy(pages[c][:].indirect(l7[:]), p_sb[:])
+            else:
+                nc.scalar.copy(p_sb[:], p_ps[:])
+                nc.scalar.activation(pages[c][:].indirect(l7[:]), p_sb[:], ACT.Copy)
+            nc.sync.dma_start(out[cols, :], pages[c][:])

@@ -21,6 +21,7 @@ P = 128
 PACK = 4
 QUADS = 4
 QUAD = 32
+HALF = 64
 ROWS = 4
 WIDE = 512
 
@@ -40,32 +41,41 @@ def tile_list_leadmeetthenlook_twow_store_scattered_kernel(
             nc.sync.dma_start(tile[:], src)
             return tile
 
-        def by_quad(scales):
-            return scales[0].bitcast(I32).rearrange("(q r) c -> r q c", r=ROWS)
+        def quad_pair(scales, q):
+            return scales[0].bitcast(I32).rearrange("(h q r) c -> q r h c", h=2, q=2)[q]
 
         xs_plane = keep.tile([P, T], U8, name="xs_plane", align_bytes=64)
-        ws_plane = keep.tile([P, 2, R], U8, name="ws_plane", align_bytes=64)
+        ws_plane = keep.tile([P, 2, 2, R // 4], I32, name="ws_plane", align_bytes=64)
         vs_plane = keep.tile([P, S], U8, name="vs_plane", align_bytes=64)
-        nc.vector.memset(xs_plane[:].bitcast(I32), 0)
-        nc.vector.memset(ws_plane[:].rearrange("p a c -> p (a c)").bitcast(I32), 0)
-        nc.vector.memset(vs_plane[:].bitcast(I32), 0)
         pages = [keep.tile([P, E], F32, name="page%d" % c) for c in range(2)]
+        nc.gpsimd.memset(xs_plane[:].bitcast(I32), 0)
+        nc.vector.memset(ws_plane[HALF:], 0)
+        nc.vector.memset(vs_plane[:].bitcast(I32), 0)
         nc.vector.memset(pages[0][:], 0.0)
         nc.gpsimd.memset(pages[1][:], 0.0)
 
-        xs_stage = keep.tile([P, 2, T // 4], I32, name="xs_stage")
-        for h in range(2):
-            nc.sync.dma_start(xs_stage[64 * h : 64 * h + ROWS, :, :], by_quad(xt_scales)[:, 2 * h : 2 * h + 2, :])
+        def load_plane(plane, scales):
+            for q in range(QUADS):
+                nc.sync.dma_start(
+                    plane[QUAD * q : QUAD * q + ROWS, :].bitcast(I32),
+                    scales[0, ROWS * q : ROWS * q + ROWS, :].bitcast(I32),
+                )
+
+        def load_w_scales(q):
+            rows = slice(HALF + QUAD * q, HALF + QUAD * q + ROWS)
+            nc.sync.dma_start(ws_plane[rows, :, 0, :], quad_pair(w_scales, q))
+            nc.sync.dma_start(ws_plane[rows, :, 1, :], quad_pair(w2_scales, q))
+
         l1 = load_list(offs, "l1")
+        load_plane(xs_plane, xt_scales)
         xt_sb = keep.tile([P, T], U16, name="xt_sb", align_bytes=64)
         nc.sync.dma_start(xt_sb[:].bitcast(I32), xt_words[0].bitcast(I32))
-        ws_stage = keep.tile([ROWS, QUADS, 2, R // 4], I32, name="ws_stage")
-        nc.sync.dma_start(ws_stage[:, :, 0, :], by_quad(w_scales))
-        nc.sync.dma_start(ws_stage[:, :, 1, :], by_quad(w2_scales))
         w_sb = keep.tile([P, R], U32, name="w_sb")
         w2_sb = keep.tile([P, R], U32, name="w2_sb")
         nc.sync.dma_start(w_sb[:].bitcast(I32), w_words[0].rearrange("p n t -> p (n t)").bitcast(I32))
         nc.sync.dma_start(w2_sb[:].bitcast(I32), w2_words[0].rearrange("p n t -> p (n t)").bitcast(I32))
+        load_w_scales(0)
+        load_w_scales(1)
         l2 = load_list(offs2, "l2")
         l3 = load_list(offs3, "l3")
         l6 = load_list(offs6, "l6")
@@ -73,36 +83,26 @@ def tile_list_leadmeetthenlook_twow_store_scattered_kernel(
         nc.sync.dma_start(vs_sb[:].bitcast(I32), vs_words[0].bitcast(I32))
         l4 = load_list(offs4, "l4")
         l5 = load_list(offs5, "l5")
-        for q in range(QUADS):
-            nc.sync.dma_start(
-                vs_plane[QUAD * q : QUAD * q + ROWS, :].bitcast(I32),
-                vs_scales[0, ROWS * q : ROWS * q + ROWS, :].bitcast(I32),
-            )
+        load_plane(vs_plane, vs_scales)
         l7 = load_list(offs7, "l7")
 
-        for q in range(QUADS):
-            src = 64 * (q // 2)
-            nc.vector.tensor_copy(
-                xs_plane[QUAD * q : QUAD * q + ROWS, :].bitcast(I32), xs_stage[src : src + ROWS, q % 2, :]
-            )
-        xg_scales = keep.tile([P, J], U8, name="xg_scales", align_bytes=64)
-        xg_words = keep.tile([P, J], U16, name="xg_words", align_bytes=64)
-        nc.vector.tensor_copy(xg_scales[:], xs_plane[:].indirect(l1[:]))
-        for q in range(QUADS):
-            nc.vector.tensor_copy(
-                ws_plane[QUAD * q : QUAD * q + ROWS, :, :].rearrange("p a c -> p (a c)").bitcast(I32),
-                ws_stage[:, q, :, :].rearrange("p a c -> p (a c)"),
-            )
+        xg_scales = keep.tile([P, J], U8, name="xg_scales", tag="picked_scales", align_bytes=64)
+        xg_words = keep.tile([P, J], U16, name="xg_words", tag="picked_words", align_bytes=64)
         nc.vector.tensor_copy(xg_words[:], xt_sb[:].indirect(l1[:]))
+        nc.vector.tensor_copy(xg_scales[:], xs_plane[:].indirect(l1[:]))
+        nc.vector.tensor_copy(
+            ws_plane[:HALF, 1, :, :].rearrange("p a c -> p (a c)"),
+            ws_plane[HALF:, 0, :, :].rearrange("p a c -> p (a c)"),
+        )
 
         w_dealt = keep.tile([P, PACK, P], U32, name="w_dealt", align_bytes=64)
         w2_dealt = keep.tile([P, PACK, P], U32, name="w2_dealt", align_bytes=64)
         ws_dealt = keep.tile([P, PACK, 2, P], U8, name="ws_dealt", align_bytes=64)
-        nc.scalar.copy(w_dealt[:], w_sb[:].rearrange("p (m t) -> p t m", t=PACK))
+        nc.scalar.copy(w_dealt[:].rearrange("p t m -> p m t"), w_sb[:].rearrange("p (m t) -> p m t", t=PACK))
         w2_view = w2_sb[:].rearrange("p (m t) -> p t m", t=PACK)
         nc.scalar.copy(w2_dealt[:, 0, :], w2_view[:, 0, :])
-        nc.scalar.copy(w2_dealt[:, 1:, :], w2_view[:, 1:, :])
-        ws_view = ws_plane[:].rearrange("p a (m t) -> p t a m", t=PACK)
+        nc.scalar.copy(w2_dealt[:, 1:, :].rearrange("p t m -> p m t"), w2_view[:, 1:, :].rearrange("p t m -> p m t"))
+        ws_view = ws_plane[:, 1, :, :].bitcast(U8).rearrange("p a (m t) -> p t a m", t=PACK)
         nc.vector.tensor_copy(ws_dealt[:, 0, :, :], ws_view[:, 0, :, :])
         nc.vector.tensor_copy(ws_dealt[:, 1:, :, :], ws_view[:, 1:, :, :])
 
@@ -128,9 +128,10 @@ def tile_list_leadmeetthenlook_twow_store_scattered_kernel(
             a_sb.append(a_t)
             b_sb.append(b_t)
 
-        vg_scales = keep.tile([P, N], U8, name="vg_scales", align_bytes=64)
-        vg_words = keep.tile([P, N], U16, name="vg_words", align_bytes=64)
+        vg_scales = keep.tile([P, N], U8, name="vg_scales", tag="picked_scales", align_bytes=64)
+        vg_words = keep.tile([P, N], U16, name="vg_words", tag="picked_words", align_bytes=64)
         nc.vector.tensor_copy(vg_words[:], vs_sb[:].indirect(l6[:]))
+        nc.vector.tensor_copy(vg_scales[:], vs_plane[:].indirect(l6[:]))
 
         diff = keep.tile([P, PACK, O], F32, name="diff")
         for t in range(PACK):
@@ -138,18 +139,23 @@ def tile_list_leadmeetthenlook_twow_store_scattered_kernel(
             gb = keep.tile([P, I], F32, name="gb%d" % t)
             nc.scalar.activation(ga[:], a_sb[t][:].indirect(l2[:]), ACT.Copy, scale=b_sb[t][:, 0:1])
             nc.scalar.activation(gb[:], b_sb[t][:].indirect(l3[:]), ACT.Copy, scale=a_sb[t][:, 0:1])
-            h1 = keep.tile([P, I], F32, name="h1_%d" % t)
+            h1 = keep.tile([P, I], F32, name="h1_%d" % t, tag="h1", bufs=2)
             nc.vector.tensor_tensor(h1[:], ga[:], gb[:], ALU.max)
             first = keep.tile([P, O], F32, name="first%d" % t)
-            nc.vector.tensor_copy(first[:], h1[:].indirect(l4[:]))
+            if t == PACK - 1:
+                nc.scalar.activation(first[:], h1[:].indirect(l4[:]), ACT.Copy)
+            else:
+                nc.vector.tensor_copy(first[:], h1[:].indirect(l4[:]))
             nc.vector.tensor_tensor(diff[:, t, :], h1[:].indirect(l5[:]), first[:], ALU.subtract)
 
-        nc.vector.tensor_copy(vg_scales[:], vs_plane[:].indirect(l6[:]))
-
         hid = keep.tile([P, O, PACK], BF16, name="hid", align_bytes=64)
-        nc.scalar.activation(
-            hid[:].rearrange("p (c i) t -> p c t i", i=4), diff[:].rearrange("p t (c i) -> p c t i", i=4), ACT.Abs
-        )
+        for u in range(2):
+            pair = slice(2 * u, 2 * u + 2)
+            nc.scalar.activation(
+                hid[:, :, pair].rearrange("p (c i) t -> p c t i", i=4),
+                diff[:, pair, :].rearrange("p t (c i) -> p c t i", i=4),
+                ACT.Abs,
+            )
         hid_words = keep.tile([P, O], U32, name="hid_words", align_bytes=64)
         hid_scales = keep.tile([P, O], U8, name="hid_scales", align_bytes=64)
         nc.vector.quantize_mx(

@@ -103,17 +103,17 @@ def tile_list_leadmeetthenlook_twow_store_scattered_kernel(
         nc.scalar.copy(w2_dealt[:, 0, :], w2_view[:, 0, :])
         nc.scalar.copy(w2_dealt[:, 1:, :].rearrange("p t m -> p m t"), w2_view[:, 1:, :].rearrange("p t m -> p m t"))
         ws_view = ws_plane[:, 1, :, :].bitcast(U8).rearrange("p a (m t) -> p t a m", t=PACK)
-        nc.vector.tensor_copy(ws_dealt[:, 0, :, :], ws_view[:, 0, :, :])
-        nc.vector.tensor_copy(ws_dealt[:, 1:, :, :], ws_view[:, 1:, :, :])
 
         a_sb, b_sb = [], []
         for t in range(PACK):
             a_ps = psum.tile([P, J], F32, name="a_ps%d" % t, tag="bank_a%d" % t)
             b_ps = psum.tile([P, J], F32, name="b_ps%d" % t, tag="bank_b%d" % t)
+            nc.vector.tensor_copy(ws_dealt[:, t, 0, :], ws_view[:, t, 0, :])
             nc.tensor.matmul_mx(
                 out=a_ps[:], lhsT=w_dealt[:, t, :].bitcast(E4M3), lhsT_scale=ws_dealt[:, t, 0, :],
                 rhs=xg_words[:].bitcast(E2M1), rhs_scale=xg_scales[:], start=True, stop=True,
             )
+            nc.vector.tensor_copy(ws_dealt[:, t, 1, :], ws_view[:, t, 1, :])
             nc.tensor.matmul_mx(
                 out=b_ps[:], lhsT=w2_dealt[:, t, :].bitcast(E5M2), lhsT_scale=ws_dealt[:, t, 1, :],
                 rhs=xg_words[:].bitcast(E2M1), rhs_scale=xg_scales[:], start=True, stop=True,
@@ -122,6 +122,8 @@ def tile_list_leadmeetthenlook_twow_store_scattered_kernel(
             b_t = keep.tile([P, WIDE], F32, name="b_sb%d" % t)
             if t == 0:
                 nc.scalar.copy(a_t[:, :J], a_ps[:])
+                lb0 = keep.tile([P, 1], F32, name="lb0")
+                nc.vector.tensor_copy(lb0[:], b_ps[:, 0:1])
             else:
                 nc.vector.tensor_copy(a_t[:, :J], a_ps[:])
             nc.vector.tensor_copy(b_t[:, :J], b_ps[:])
@@ -137,18 +139,23 @@ def tile_list_leadmeetthenlook_twow_store_scattered_kernel(
         for t in range(PACK):
             ga = keep.tile([P, I], F32, name="ga%d" % t)
             gb = keep.tile([P, I], F32, name="gb%d" % t)
-            nc.scalar.activation(ga[:], a_sb[t][:].indirect(l2[:]), ACT.Copy, scale=b_sb[t][:, 0:1])
+            nc.scalar.activation(ga[:], a_sb[t][:].indirect(l2[:]), ACT.Copy, scale=lb0[:] if t == 0 else b_sb[t][:, 0:1])
             nc.scalar.activation(gb[:], b_sb[t][:].indirect(l3[:]), ACT.Copy, scale=a_sb[t][:, 0:1])
-            h1 = keep.tile([P, I], F32, name="h1_%d" % t, tag="h1", bufs=2)
+            h1 = keep.tile([P, I], F32, name="h1_%d" % t, tag="h1", bufs=2, align_bytes=64)
             nc.vector.tensor_tensor(h1[:], ga[:], gb[:], ALU.max)
             first = keep.tile([P, O], F32, name="first%d" % t)
-            if t == PACK - 1:
+            if t >= 2:
                 nc.scalar.activation(first[:], h1[:].indirect(l4[:]), ACT.Copy)
             else:
                 nc.vector.tensor_copy(first[:], h1[:].indirect(l4[:]))
-            nc.vector.tensor_tensor(diff[:, t, :], h1[:].indirect(l5[:]), first[:], ALU.subtract)
+            if t == PACK - 1:
+                second = keep.tile([P, O], F32, name="second")
+                nc.vector.tensor_copy(second[:], h1[:].indirect(l5[:]))
+                nc.vector.tensor_tensor(diff[:, t, :], second[:], first[:], ALU.subtract)
+            else:
+                nc.vector.tensor_tensor(diff[:, t, :], h1[:].indirect(l5[:]), first[:], ALU.subtract)
 
-        hid = keep.tile([P, O, PACK], BF16, name="hid", align_bytes=64)
+        hid = keep.tile([P, O, PACK], BF16, name="hid", tag="h1", bufs=2, align_bytes=64)
         for u in range(2):
             pair = slice(2 * u, 2 * u + 2)
             nc.scalar.activation(
@@ -170,10 +177,10 @@ def tile_list_leadmeetthenlook_twow_store_scattered_kernel(
                 rhs=hid_words[:].bitcast(E5M2), rhs_scale=hid_scales[:], start=True, stop=True,
             )
             p_sb = keep.tile([P, O], F32, name="p_sb%d" % c)
-            if c == 0:
+            if c == 1:
                 nc.vector.tensor_copy(p_sb[:], p_ps[:])
                 nc.vector.tensor_copy(pages[c][:].indirect(l7[:]), p_sb[:])
             else:
                 nc.scalar.copy(p_sb[:], p_ps[:])
                 nc.scalar.activation(pages[c][:].indirect(l7[:]), p_sb[:], ACT.Copy)
-            nc.sync.dma_start(out[cols, :], pages[c][:])
+            (nc.sync if c == 1 else nc.scalar).dma_start(out[cols, :], pages[c][:])

from contextlib import ExitStack

import concourse.mybir as mybir

K, T, J, R, I, O, N, S, E = 512, 1024, 256, 512, 256, 128, 256, 1024, 1024
FLOPS = 2 * (2 * K * R * J + R * N * O)

F32 = mybir.dt.float32
BF16 = mybir.dt.bfloat16
I32 = mybir.dt.int32
U32 = mybir.dt.uint32
U16 = mybir.dt.uint16
U8 = mybir.dt.uint8
E4M3 = mybir.dt.float8_e4m3fn_x4
E5M2 = mybir.dt.float8_e5m2_x4
E2M1 = mybir.dt.float4_e2m1fn_x4
ACT = mybir.ActivationFunctionType
ALU = mybir.AluOpType

P = 128
PACK = 4
QUADS = 4
QUAD = 32
HALF = 64
ROWS = 4
WIDE = 512


def tile_list_leadmeetthenlook_twow_store_scattered_kernel(
    tc, xt_words, xt_scales, w_words, w_scales, w2_words, w2_scales, vs_words, vs_scales,
    offs, offs2, offs3, offs4, offs5, offs6, offs7, out,
):
    nc = tc.nc
    with ExitStack() as ctx:
        lists = ctx.enter_context(tc.tile_pool(name="lists", bufs=1))
        keep = ctx.enter_context(tc.tile_pool(name="keep", bufs=1))
        psum = ctx.enter_context(tc.psum_pool(name="psum", bufs=1))

        def load_list(src, name):
            tile = lists.tile(list(src.shape), U16, name=name)
            nc.sync.dma_start(tile[:], src)
            return tile

        def quad_pair(scales, q):
            return scales[0].bitcast(I32).rearrange("(h q r) c -> q r h c", h=2, q=2)[q]

        xs_plane = keep.tile([P, T], U8, name="xs_plane", align_bytes=64)
        ws_plane = keep.tile([P, 2, 2, R // 4], I32, name="ws_plane", align_bytes=64)
        vs_plane = keep.tile([P, S], U8, name="vs_plane", align_bytes=64)
        pages = [keep.tile([P, E], F32, name="page%d" % c) for c in range(2)]
        nc.gpsimd.memset(xs_plane[:].bitcast(I32), 0)
        nc.vector.memset(ws_plane[HALF:], 0)
        nc.vector.memset(vs_plane[:].bitcast(I32), 0)
        nc.vector.memset(pages[0][:], 0.0)
        nc.gpsimd.memset(pages[1][:], 0.0)

        def load_plane(plane, scales):
            for q in range(QUADS):
                nc.sync.dma_start(
                    plane[QUAD * q : QUAD * q + ROWS, :].bitcast(I32),
                    scales[0, ROWS * q : ROWS * q + ROWS, :].bitcast(I32),
                )

        def load_w_scales(q):
            rows = slice(HALF + QUAD * q, HALF + QUAD * q + ROWS)
            nc.sync.dma_start(ws_plane[rows, :, 0, :], quad_pair(w_scales, q))
            nc.sync.dma_start(ws_plane[rows, :, 1, :], quad_pair(w2_scales, q))

        l1 = load_list(offs, "l1")
        load_plane(xs_plane, xt_scales)
        xt_sb = keep.tile([P, T], U16, name="xt_sb", align_bytes=64)
        nc.sync.dma_start(xt_sb[:].bitcast(I32), xt_words[0].bitcast(I32))
        w_sb = keep.tile([P, R], U32, name="w_sb")
        w2_sb = keep.tile([P, R], U32, name="w2_sb")
        nc.sync.dma_start(w_sb[:].bitcast(I32), w_words[0].rearrange("p n t -> p (n t)").bitcast(I32))
        nc.sync.dma_start(w2_sb[:].bitcast(I32), w2_words[0].rearrange("p n t -> p (n t)").bitcast(I32))
        load_w_scales(0)
        load_w_scales(1)
        l2 = load_list(offs2, "l2")
        l3 = load_list(offs3, "l3")
        l6 = load_list(offs6, "l6")
        vs_sb = keep.tile([P, S], U16, name="vs_sb", align_bytes=64)
        nc.sync.dma_start(vs_sb[:].bitcast(I32), vs_words[0].bitcast(I32))
        l4 = load_list(offs4, "l4")
        l5 = load_list(offs5, "l5")
        load_plane(vs_plane, vs_scales)
        l7 = load_list(offs7, "l7")

        xg_scales = keep.tile([P, J], U8, name="xg_scales", tag="picked_scales", align_bytes=64)
        xg_words = keep.tile([P, J], U16, name="xg_words", tag="picked_words", align_bytes=64)
        nc.vector.tensor_copy(xg_words[:], xt_sb[:].indirect(l1[:]))
        nc.vector.tensor_copy(xg_scales[:], xs_plane[:].indirect(l1[:]))
        nc.vector.tensor_copy(
            ws_plane[:HALF, 1, :, :].rearrange("p a c -> p (a c)"),
            ws_plane[HALF:, 0, :, :].rearrange("p a c -> p (a c)"),
        )

        w_dealt = keep.tile([P, PACK, P], U32, name="w_dealt", align_bytes=64)
        w2_dealt = keep.tile([P, PACK, P], U32, name="w2_dealt", align_bytes=64)
        ws_dealt = keep.tile([P, PACK, 2, P], U8, name="ws_dealt", align_bytes=64)
        nc.scalar.copy(w_dealt[:].rearrange("p t m -> p m t"), w_sb[:].rearrange("p (m t) -> p m t", t=PACK))
        w2_view = w2_sb[:].rearrange("p (m t) -> p t m", t=PACK)
        nc.scalar.copy(w2_dealt[:, 0, :], w2_view[:, 0, :])
        nc.scalar.copy(w2_dealt[:, 1:, :].rearrange("p t m -> p m t"), w2_view[:, 1:, :].rearrange("p t m -> p m t"))
        ws_view = ws_plane[:, 1, :, :].bitcast(U8).rearrange("p a (m t) -> p t a m", t=PACK)

        a_sb, b_sb = [], []
        for t in range(PACK):
            a_ps = psum.tile([P, J], F32, name="a_ps%d" % t, tag="bank_a%d" % t)
            b_ps = psum.tile([P, J], F32, name="b_ps%d" % t, tag="bank_b%d" % t)
            nc.vector.tensor_copy(ws_dealt[:, t, 0, :], ws_view[:, t, 0, :])
            nc.tensor.matmul_mx(
                out=a_ps[:], lhsT=w_dealt[:, t, :].bitcast(E4M3), lhsT_scale=ws_dealt[:, t, 0, :],
                rhs=xg_words[:].bitcast(E2M1), rhs_scale=xg_scales[:], start=True, stop=True,
            )
            nc.vector.tensor_copy(ws_dealt[:, t, 1, :], ws_view[:, t, 1, :])
            nc.tensor.matmul_mx(
                out=b_ps[:], lhsT=w2_dealt[:, t, :].bitcast(E5M2), lhsT_scale=ws_dealt[:, t, 1, :],
                rhs=xg_words[:].bitcast(E2M1), rhs_scale=xg_scales[:], start=True, stop=True,
            )
            a_t = keep.tile([P, WIDE], F32, name="a_sb%d" % t)
            b_t = keep.tile([P, WIDE], F32, name="b_sb%d" % t)
            if t == 0:
                nc.scalar.copy(a_t[:, :J], a_ps[:])
                lb0 = keep.tile([P, 1], F32, name="lb0")
                nc.vector.tensor_copy(lb0[:], b_ps[:, 0:1])
            else:
                nc.vector.tensor_copy(a_t[:, :J], a_ps[:])
            nc.vector.tensor_copy(b_t[:, :J], b_ps[:])
            a_sb.append(a_t)
            b_sb.append(b_t)

        vg_scales = keep.tile([P, N], U8, name="vg_scales", tag="picked_scales", align_bytes=64)
        vg_words = keep.tile([P, N], U16, name="vg_words", tag="picked_words", align_bytes=64)
        nc.vector.tensor_copy(vg_words[:], vs_sb[:].indirect(l6[:]))
        nc.vector.tensor_copy(vg_scales[:], vs_plane[:].indirect(l6[:]))

        diff = keep.tile([P, PACK, O], F32, name="diff")
        for t in range(PACK):
            ga = keep.tile([P, I], F32, name="ga%d" % t)
            gb = keep.tile([P, I], F32, name="gb%d" % t)
            nc.scalar.activation(ga[:], a_sb[t][:].indirect(l2[:]), ACT.Copy, scale=lb0[:] if t == 0 else b_sb[t][:, 0:1])
            nc.scalar.activation(gb[:], b_sb[t][:].indirect(l3[:]), ACT.Copy, scale=a_sb[t][:, 0:1])
            h1 = keep.tile([P, I], F32, name="h1_%d" % t, tag="h1", bufs=2, align_bytes=64)
            nc.vector.tensor_tensor(h1[:], ga[:], gb[:], ALU.max)
            first = keep.tile([P, O], F32, name="first%d" % t)
            if t >= 2:
                nc.scalar.activation(first[:], h1[:].indirect(l4[:]), ACT.Copy)
            else:
                nc.vector.tensor_copy(first[:], h1[:].indirect(l4[:]))
            if t == PACK - 1:
                second = keep.tile([P, O], F32, name="second")
                nc.vector.tensor_copy(second[:], h1[:].indirect(l5[:]))
                nc.vector.tensor_tensor(diff[:, t, :], second[:], first[:], ALU.subtract)
            else:
                nc.vector.tensor_tensor(diff[:, t, :], h1[:].indirect(l5[:]), first[:], ALU.subtract)

        hid = keep.tile([P, O, PACK], BF16, name="hid", tag="h1", bufs=2, align_bytes=64)
        for u in range(2):
            pair = slice(2 * u, 2 * u + 2)
            nc.scalar.activation(
                hid[:, :, pair].rearrange("p (c i) t -> p c t i", i=4),
                diff[:, pair, :].rearrange("p t (c i) -> p c t i", i=4),
                ACT.Abs,
            )
        hid_words = keep.tile([P, O], U32, name="hid_words", align_bytes=64)
        hid_scales = keep.tile([P, O], U8, name="hid_scales", align_bytes=64)
        nc.vector.quantize_mx(
            out=hid_words[:].bitcast(E5M2), scales=hid_scales[:], in_=hid[:].rearrange("p o t -> p (o t)")
        )

        for c in range(2):
            cols = slice(c * P, (c + 1) * P)
            p_ps = psum.tile([P, O], F32, name="p_ps%d" % c, tag="bank_a%d" % c)
            nc.tensor.matmul_mx(
                out=p_ps[:], lhsT=vg_words[:, cols].bitcast(E2M1), lhsT_scale=vg_scales[:, cols],
                rhs=hid_words[:].bitcast(E5M2), rhs_scale=hid_scales[:], start=True, stop=True,
            )
            p_sb = keep.tile([P, O], F32, name="p_sb%d" % c)
            if c == 1:
                nc.vector.tensor_copy(p_sb[:], p_ps[:])
                nc.vector.tensor_copy(pages[c][:].indirect(l7[:]), p_sb[:])
            else:
                nc.scalar.copy(p_sb[:], p_ps[:])
                nc.scalar.activation(pages[c][:].indirect(l7[:]), p_sb[:], ACT.Copy)
            (nc.sync if c == 1 else nc.scalar).dma_start(out[cols, :], pages[c][:])
